import numpy as np, ml_dtypes
CORES = [56,64,184,192,312,320,440,448]
N = 8
F = 32
def setup_inputs(rng):
    m = (rng.standard_normal((N, 128, 128), dtype=np.float32) / 11).astype(ml_dtypes.bfloat16)
    return {"m": m, "mt": m.transpose(0, 2, 1).copy(), "x": rng.standard_normal((N, 128, F), dtype=np.float32).astype(ml_dtypes.bfloat16)}
def setup_inputs_big(rng):
    d = setup_inputs(rng)
    for k in ("x",): d[k] = (d[k].astype(np.float32) * 1048576.0).astype(d[k].dtype)
    return d
def setup_inputs_small(rng):
    d = setup_inputs(rng)
    for k in ("x",): d[k] = (d[k].astype(np.float32) * (1 / 1048576.0)).astype(d[k].dtype)
    return d
def setup_inputs_apart(rng):
    d = setup_inputs(rng)
    f = (10.0 ** rng.permutation(np.linspace(-1.5, 1.5, N))).astype(np.float32).reshape(N, 1, 1)
    for k in ("x",): d[k] = (d[k].astype(np.float32) * f).astype(d[k].dtype)
    return d
def reference(m, mt, x):
    M, X = m.astype(np.float64), x.astype(np.float64)
    y = np.zeros((N, 128, F)); p = X[0]
    for r in range(N):
        p = M[r].T @ p
        y[r] = p
    return {"y": y.astype(ml_dtypes.bfloat16)}

@@ -1,0 +1,218 @@
+from concourse.bass import DstId, RemoteDMATransfer
+
+P, F = 128, 32
+W0 = P + F
+SRC_ENGINES = 8
+FWD_ENGINES = 8
+
+SCRATCH = {
+    "d": ("dram", [P, P], "bfloat16"),
+    "d0": ("dram", [P, W0], "bfloat16"),
+    "l0": ("sbuf", [P, W0], "bfloat16"),
+    "lm": ("sbuf", [P, 6 * P], "bfloat16"),
+    "own": ("sbuf", [P, P], "bfloat16"),
+    "pr": ("sbuf", [P, 4 * P], "bfloat16"),
+    "pv": ("sbuf", [P, 4 * F], "bfloat16"),
+    "pn": ("psum", [P, 512], "float32"),
+    "pw0": ("psum", [P, 512], "float32"),
+    "pw1": ("psum", [P, 512], "float32"),
+    "pw2": ("psum", [P, 512], "float32"),
+    "pw3": ("psum", [P, 512], "float32"),
+}
+SEMAPHORES = (["arr%d" % s for s in range(7)] + ["mm%d" % i for i in range(8)] + ["cp%d" % i for i in range(8)]
+              + ["staged", "mine", "sent", "stored"])
+
+_CACHE = {}
+
+
+def _links(topo, a, b):
+    if topo.host(a) == topo.host(b) and topo.chip(a) == topo.chip(b):
+        return 0
+    if topo.rack(topo.host(a)) != topo.rack(topo.host(b)):
+        twin = topo.host(a) * topo.CORES_PER_HOST + b % topo.CORES_PER_HOST
+        return 1 + _links(topo, a, twin)
+    if topo.mates(a, b) or topo.same_plane(a, b):
+        return 1
+    return 2
+
+
+def _plan(cores, topo):
+    n = len(cores)
+    world = range((max(topo.host(c) for c in cores) + 1) * topo.CORES_PER_HOST)
+    used = set(cores)
+    route, into, outof, pending = {}, {}, {}, []
+    for s in range(n - 1):
+        for d in range(s + 1, n):
+            if topo.may_write(cores[s], cores[d]):
+                route[(s, d)] = None
+                k = (d, topo.die(cores[s]))
+                into[k] = into.get(k, 0) + 1
+            else:
+                cand = [c for c in world if c not in used and topo.may_write(cores[s], c) and topo.may_write(c, cores[d])]
+                onchip = any(_links(topo, cores[s], c) == 0 for c in cand)
+                pending.append((0 if onchip else 1, len(cand), -d, s, d))
+    for _, _, _, s, d in sorted(pending):
+        a, b = cores[s], cores[d]
+        best = None
+        for c in world:
+            if c in used or not (topo.may_write(a, c) and topo.may_write(c, b)):
+                continue
+            la, lb = _links(topo, a, c), _links(topo, c, b)
+            key = ((la > 0) + (lb > 0), la + lb, into.get((d, topo.die(c)), 0),
+                   outof.get((topo.host(c), topo.chip(c), topo.die(c)), 0), c)
+            if best is None or key < best:
+                best = key
+        c = best[-1]
+        used.add(c)
+        route[(s, d)] = c
+        into[(d, topo.die(c))] = into.get((d, topo.die(c)), 0) + 1
+        k = (topo.host(c), topo.chip(c), topo.die(c))
+        outof[k] = outof.get(k, 0) + 1
+    return route
+
+
+def _engines(mask, n):
+    out, cnt, bit = 0, 0, 1
+    while bit <= mask and cnt < n:
+        if mask & bit:
+            out |= bit
+            cnt += 1
+        bit <<= 1
+    return out, cnt
+
+
+def _src_mask(topo, src, dsts):
+    m = topo.mask(src, dsts[0])
+    for c in dsts[1:]:
+        m &= topo.mask(src, c)
+    return _engines(m, SRC_ENGINES)
+
+
+def _sender_calls(cores, route, topo, s):
+    later = [d for d in range(len(cores) - 1, s, -1)]
+    via = [route[(s, d)] for d in later if route[(s, d)] is not None]
+    straight = [cores[d] for d in later if route[(s, d)] is None]
+    calls = []
+    for dsts, relay in ((via, True), (straight, False)):
+        if dsts:
+            mask, cnt = _src_mask(topo, cores[s], dsts)
+            calls.append((dsts, relay, mask, cnt))
+    return calls
+
+
+def _landing(T, s):
+    return T.l0[:] if s == 0 else T.lm[:, (s - 1) * P:s * P]
+
+
+def _stage(T, s):
+    return T.d0[:] if s == 0 else T.d[:]
+
+
+def rank_program(g, core, T, topo):
+    cores = list(T.cores)
+    if "route" not in _CACHE:
+        _CACHE["route"] = _plan(cores, topo)
+    route = _CACHE["route"]
+    n = len(cores)
+    rank = T.rank_of(core)
+
+    if rank is None:
+        for (s, d), c in route.items():
+            if c != core:
+                continue
+            got = [cnt for dsts, relay, _, cnt in _sender_calls(cores, route, topo, s) if relay][0]
+            mask, cnt = _engines(topo.mask(core, cores[d]), FWD_ENGINES)
+            rid, pid = topo.addr(cores[d], core)
+            g.wait_ge(T.sem["arr%d" % s], got)
+            g.remote_dma(_landing(T, s), _stage(T, s), T.sem["arr%d" % s], T.sem.sent, pid, rid, mask)
+            g.wait_ge(T.sem.sent, cnt)
+        return
+
+    if rank == 0:
+        g.sync.dma_start(T.d0[:, 0:P], T.m[:]).then_inc(T.sem.staged, 16)
+        g.scalar.dma_start(T.d0[:, P:W0], T.x[:]).then_inc(T.sem.staged, 16)
+        g.sync.dma_start(T.l0[:, 0:P], T.m[:]).then_inc(T.sem.mine, 16)
+        g.scalar.dma_start(T.l0[:, P:W0], T.x[:]).then_inc(T.sem.mine, 16)
+        staged, mine = 32, 32
+    else:
+        if rank < n - 1:
+            g.sync.dma_start(T.d[:], (T.mt if rank % 2 else T.m)[:]).then_inc(T.sem.staged, 16)
+        g.scalar.dma_start(T.own[:], T.m[:]).then_inc(T.sem.mine, 16)
+        staged, mine = 16, 16
+
+    sent = 0
+    if rank < n - 1:
+        g.wait_ge(T.sem.staged, staged)
+        for dsts, relay, mask, cnt in _sender_calls(cores, route, topo, rank):
+            ids = []
+            for c in dsts:
+                rid, pid = topo.addr(c, core)
+                ids.append(DstId(rid=rid, pnc=pid))
+            out = _stage(T, rank) if relay else _landing(T, rank)
+            g.remote_dma_fused([RemoteDMATransfer(dst_ids=ids, dma_engine_mask=mask, remote_sem=T.sem["arr%d" % rank],
+                                                  srcs=[_stage(T, rank)], dsts=[out for _ in dsts])],
+                               local_sem=T.sem.sent)
+            sent += cnt
+
+    def arrival(s):
+        if s == rank or (s == 0 and rank == 0):
+            return ("mine", mine)
+        c = route[(s, rank)]
+        if c is None:
+            cnt = [k for dsts, relay, _, k in _sender_calls(cores, route, topo, s) if not relay][0]
+        else:
+            cnt = _engines(topo.mask(c, core), FWD_ENGINES)[1]
+        return ("arr%d" % s, cnt)
+
+    def mat(s):
+        if s == rank:
+            return T.own[:], [arrival(s)]
+        return T.lm[:, (s - 1) * P:s * P], [arrival(s)]
+
+    ops = []
+
+    def product(lhsT, rhs, wide):
+        i = len(ops)
+        k = sum(1 for o in ops if o[2] == wide)
+        if wide:
+            ps, sb = T["pw%d" % k][:, 0:P], T.pr[:, k * P:(k + 1) * P]
+        else:
+            ps, sb = T.pn[:, 0:F], T.pv[:, k * F:(k + 1) * F]
+        ops.append((lhsT, rhs, wide, ps, sb))
+        return sb, [("cp%d" % i, 1)]
+
+    a0 = [arrival(0)]
+    p = product((T.l0[:, 0:P], a0), (T.l0[:, P:W0], a0), False)
+    pairs = []
+    for j in range(1, rank // 2 + 1):
+        if rank % 2 and 2 * j == rank - 1 and rank >= 7:
+            pairs.append(product(mat(2 * j), mat(2 * j - 1), True))
+        else:
+            pairs.append(product(mat(2 * j - 1), mat(2 * j), True))
+    tail_done = False
+    for j, b in enumerate(pairs):
+        if rank % 2 and rank >= 7 and j == len(pairs) - 1:
+            p = product(tail, p, False)
+            tail_done = True
+            break
+        p = product(b, p, False)
+        if rank % 2 and rank >= 7 and j == 0:
+            tail = product(pairs[-1], mat(rank), True)
+    if rank % 2 and not tail_done:
+        p = product(mat(rank), p, False)
+
+    seen = set()
+    for i, (lhsT, rhs, wide, ps, sb) in enumerate(ops):
+        for w in lhsT[1] + rhs[1]:
+            if w not in seen:
+                seen.add(w)
+                g.tensor.wait_ge(T.sem[w[0]], w[1])
+        g.tensor.matmul(ps, lhsT[0], rhs[0], start=True, stop=True).then_inc(T.sem["mm%d" % i], 1)
+        g.vector.wait_ge(T.sem["mm%d" % i], 1)
+        g.vector.tensor_copy(sb, ps).then_inc(T.sem["cp%d" % i], 1)
+
+    g.sync.wait_ge(T.sem[p[1][0][0]], 1)
+    g.sync.dma_start(T.y[:], p[0]).then_inc(T.sem.stored, 16)
+    g.sync.wait_ge(T.sem.stored, 16)
+    if sent:
+        g.wait_ge(T.sem.sent, sent)

@@ -1,14 +1,13 @@
 from concourse.bass import DstId, RemoteDMATransfer
 
 P, F = 128, 32
-W0 = P + F
-SRC_ENGINES = 8
-FWD_ENGINES = 8
+ENGINES = 8
+SHARES = {1: [(0, 2)], 2: [(0, 2), (1, 3)], 3: [(0, 2), (1,), (3,)], 4: [(0,), (2,), (1,), (3,)]}
 
 SCRATCH = {
     "d": ("dram", [P, P], "bfloat16"),
-    "d0": ("dram", [P, W0], "bfloat16"),
-    "l0": ("sbuf", [P, W0], "bfloat16"),
+    "l0": ("sbuf", [P, F], "bfloat16"),
+    "xs": ("sbuf", [P, F], "bfloat16"),
     "lm": ("sbuf", [P, 6 * P], "bfloat16"),
     "own": ("sbuf", [P, P], "bfloat16"),
     "pr": ("sbuf", [P, 4 * P], "bfloat16"),
@@ -25,87 +24,130 @@ SEMAPHORES = (["arr%d" % s for s in range(7)] + ["mm%d" % i for i in range(8)] +
 _CACHE = {}
 
 
-def _links(topo, a, b):
-    if topo.host(a) == topo.host(b) and topo.chip(a) == topo.chip(b):
-        return 0
-    if topo.rack(topo.host(a)) != topo.rack(topo.host(b)):
-        twin = topo.host(a) * topo.CORES_PER_HOST + b % topo.CORES_PER_HOST
-        return 1 + _links(topo, a, twin)
-    if topo.mates(a, b) or topo.same_plane(a, b):
-        return 1
-    return 2
+def _chip(topo, c):
+    return (topo.host(c), topo.chip(c))
+
+
+def _mate(topo, a):
+    base = topo.host(a) * topo.CORES_PER_HOST
+    for c in range(base + a % topo.CORES_PER_CHIP, base + topo.CORES_PER_HOST, topo.CORES_PER_CHIP):
+        if topo.mates(a, c):
+            return c
+
+
+def _inrack(topo, a, b, die):
+    if _chip(topo, a) == _chip(topo, b):
+        return []
+    if topo.same_plane(a, b):
+        return [("out", _chip(topo, a), die), ("in", _chip(topo, b), die)]
+    return [("mate", _chip(topo, a), die)] + _inrack(topo, _mate(topo, a), b, die)
+
+
+def _way(topo, a, b):
+    die = topo.die(a)
+    if topo.rack(topo.host(a)) == topo.rack(topo.host(b)):
+        return _inrack(topo, a, b, die)
+    far = topo.host(b) * topo.CORES_PER_HOST + a % topo.CORES_PER_HOST
+    near = topo.host(a) * topo.CORES_PER_HOST + b % topo.CORES_PER_HOST
+    links = [("cable", _chip(topo, a), die)] + _inrack(topo, far, b, die)
+    if _chip(topo, near) != _chip(topo, a):
+        links += _inrack(topo, a, near, die) + [("cable", _chip(topo, near), die)]
+    return links
 
 
 def _plan(cores, topo):
     n = len(cores)
     world = range((max(topo.host(c) for c in cores) + 1) * topo.CORES_PER_HOST)
     used = set(cores)
-    route, into, outof, pending = {}, {}, {}, []
+    route, first, second, groups = {}, {}, {}, []
+
+    def fits(s, ds, c):
+        return c not in used and topo.may_write(cores[s], c) and all(topo.may_write(c, cores[d]) for d in ds)
+
     for s in range(n - 1):
-        for d in range(s + 1, n):
+        size = (F if s == 0 else P) * P * 2
+        near, far = [], []
+        for d in range(n - 1, s, -1):
             if topo.may_write(cores[s], cores[d]):
                 route[(s, d)] = None
-                k = (d, topo.die(cores[s]))
-                into[k] = into.get(k, 0) + 1
+                for k in _way(topo, cores[s], cores[d]):
+                    first[k] = first.get(k, 0) + size
+            elif any(fits(s, [d], c) and _chip(topo, c) == _chip(topo, cores[s]) for c in world):
+                near.append(d)
             else:
-                cand = [c for c in world if c not in used and topo.may_write(cores[s], c) and topo.may_write(c, cores[d])]
-                onchip = any(_links(topo, cores[s], c) == 0 for c in cand)
-                pending.append((0 if onchip else 1, len(cand), -d, s, d))
-    for _, _, _, s, d in sorted(pending):
-        a, b = cores[s], cores[d]
+                far.append(d)
+        for cls, ds in ((0, near), (1, far)):
+            for grp in ([ds] if s == 0 else [[d] for d in ds]):
+                if grp:
+                    groups.append((cls, sum(1 for c in world if fits(s, grp, c)), -grp[0], s, grp, size))
+    for _, _, _, s, grp, size in sorted(groups):
+        a = cores[s]
         best = None
         for c in world:
-            if c in used or not (topo.may_write(a, c) and topo.may_write(c, b)):
+            if not fits(s, grp, c):
                 continue
-            la, lb = _links(topo, a, c), _links(topo, c, b)
-            key = ((la > 0) + (lb > 0), la + lb, into.get((d, topo.die(c)), 0),
-                   outof.get((topo.host(c), topo.chip(c), topo.die(c)), 0), c)
-            if best is None or key < best:
-                best = key
-        c = best[-1]
+            w1 = _way(topo, a, c)
+            w2 = [k for d in grp for k in _way(topo, c, cores[d])]
+            busy = max([first.get(k, 0) for k in w1] + [0]) + max(second.get(k, 0) for k in w2)
+            key = (topo.die(c) != topo.die(a), _chip(topo, c) != _chip(topo, a),
+                   topo.rack(topo.host(c)) != topo.rack(topo.host(a)), len(w1) + len(w2), busy, c)
+            if best is None or key < best[0]:
+                best = (key, w1, w2)
+        c = best[0][-1]
         used.add(c)
-        route[(s, d)] = c
-        into[(d, topo.die(c))] = into.get((d, topo.die(c)), 0) + 1
-        k = (topo.host(c), topo.chip(c), topo.die(c))
-        outof[k] = outof.get(k, 0) + 1
+        for d in grp:
+            route[(s, d)] = c
+        for k in best[1]:
+            first[k] = first.get(k, 0) + size
+        for k in best[2]:
+            second[k] = second.get(k, 0) + size
     return route
 
 
-def _engines(mask, n):
-    out, cnt, bit = 0, 0, 1
-    while bit <= mask and cnt < n:
-        if mask & bit:
-            out |= bit
-            cnt += 1
-        bit <<= 1
-    return out, cnt
-
-
-def _src_mask(topo, src, dsts):
-    m = topo.mask(src, dsts[0])
+def _bits(topo, src, dsts):
+    mask = topo.mask(src, dsts[0])
     for c in dsts[1:]:
-        m &= topo.mask(src, c)
-    return _engines(m, SRC_ENGINES)
+        mask &= topo.mask(src, c)
+    bits, bit = [], 1
+    while bit <= mask and len(bits) < ENGINES:
+        if mask & bit:
+            bits.append(bit)
+        bit <<= 1
+    return bits
+
+
+def _together(topo, src, dsts, whole):
+    bits = _bits(topo, src, dsts)
+    if (whole and len(dsts) == 1) or len(dsts) not in SHARES:
+        return [(c, sum(bits), len(bits)) for c in dsts]
+    out = []
+    for c, quarters in zip(dsts, SHARES[len(dsts)]):
+        own = [b for q in quarters for b in bits[q::4]]
+        out.append((c, sum(own), len(own)))
+    return out
 
 
 def _sender_calls(cores, route, topo, s):
-    later = [d for d in range(len(cores) - 1, s, -1)]
-    via = [route[(s, d)] for d in later if route[(s, d)] is not None]
-    straight = [cores[d] for d in later if route[(s, d)] is None]
-    calls = []
-    for dsts, relay in ((via, True), (straight, False)):
-        if dsts:
-            mask, cnt = _src_mask(topo, cores[s], dsts)
-            calls.append((dsts, relay, mask, cnt))
+    via, straight = [], []
+    for d in range(len(cores) - 1, s, -1):
+        c = route[(s, d)]
+        if c is None:
+            straight.append(cores[d])
+        elif c not in via:
+            via.append(c)
+    calls = [(c, True, m, k) for c, m, k in (_together(topo, cores[s], via, False) if via else [])]
+    for c in straight:
+        bits = _bits(topo, cores[s], [c])
+        calls.append((c, False, sum(bits), len(bits)))
     return calls
+
+
+def _forward(cores, route, topo, s, c):
+    return _together(topo, c, [cores[d] for d in range(len(cores) - 1, s, -1) if route[(s, d)] == c], True)
 
 
 def _landing(T, s):
     return T.l0[:] if s == 0 else T.lm[:, (s - 1) * P:s * P]
-
-
-def _stage(T, s):
-    return T.d0[:] if s == 0 else T.d[:]
 
 
 def rank_program(g, core, T, topo):
@@ -116,52 +158,40 @@ def rank_program(g, core, T, topo):
     n = len(cores)
     rank = T.rank_of(core)
 
+    def write(s, src, out, dst, mask):
+        rid, pid = topo.addr(dst, core)
+        g.remote_dma(out, src, T.sem["arr%d" % s], T.sem.sent, pid, rid, mask)
+
     if rank is None:
-        for (s, d), c in route.items():
-            if c != core:
-                continue
-            got = [cnt for dsts, relay, _, cnt in _sender_calls(cores, route, topo, s) if relay][0]
-            mask, cnt = _engines(topo.mask(core, cores[d]), FWD_ENGINES)
-            rid, pid = topo.addr(cores[d], core)
+        for s in sorted(set(s for (s, d), c in route.items() if c == core)):
+            got = [k for c, _, _, k in _sender_calls(cores, route, topo, s) if c == core][0]
             g.wait_ge(T.sem["arr%d" % s], got)
-            g.remote_dma(_landing(T, s), _stage(T, s), T.sem["arr%d" % s], T.sem.sent, pid, rid, mask)
-            g.wait_ge(T.sem.sent, cnt)
+            sent = 0
+            for dst, mask, cnt in _forward(cores, route, topo, s, core):
+                write(s, T.l0[:] if s == 0 else T.d[:], _landing(T, s), dst, mask)
+                sent += cnt
+            g.wait_ge(T.sem.sent, sent)
         return
 
+    mine = 16
     if rank == 0:
-        g.sync.dma_start(T.d0[:, 0:P], T.m[:]).then_inc(T.sem.staged, 16)
-        g.scalar.dma_start(T.d0[:, P:W0], T.x[:]).then_inc(T.sem.staged, 16)
-        g.sync.dma_start(T.l0[:, 0:P], T.m[:]).then_inc(T.sem.mine, 16)
-        g.scalar.dma_start(T.l0[:, P:W0], T.x[:]).then_inc(T.sem.mine, 16)
-        staged, mine = 32, 32
+        g.sync.dma_start(T.own[:], T.m[:]).then_inc(T.sem.mine, 16)
+        g.scalar.dma_start(T.xs[:], T.x[:]).then_inc(T.sem.mine, 16)
+        mine = 32
     else:
         if rank < n - 1:
             g.sync.dma_start(T.d[:], (T.mt if rank % 2 else T.m)[:]).then_inc(T.sem.staged, 16)
+            g.scalar.wait_ge(T.sem.staged, 16)
         g.scalar.dma_start(T.own[:], T.m[:]).then_inc(T.sem.mine, 16)
-        staged, mine = 16, 16
-
-    sent = 0
-    if rank < n - 1:
-        g.wait_ge(T.sem.staged, staged)
-        for dsts, relay, mask, cnt in _sender_calls(cores, route, topo, rank):
-            ids = []
-            for c in dsts:
-                rid, pid = topo.addr(c, core)
-                ids.append(DstId(rid=rid, pnc=pid))
-            out = _stage(T, rank) if relay else _landing(T, rank)
-            g.remote_dma_fused([RemoteDMATransfer(dst_ids=ids, dma_engine_mask=mask, remote_sem=T.sem["arr%d" % rank],
-                                                  srcs=[_stage(T, rank)], dsts=[out for _ in dsts])],
-                               local_sem=T.sem.sent)
-            sent += cnt
 
     def arrival(s):
-        if s == rank or (s == 0 and rank == 0):
+        if s == rank:
             return ("mine", mine)
         c = route[(s, rank)]
         if c is None:
-            cnt = [k for dsts, relay, _, k in _sender_calls(cores, route, topo, s) if not relay][0]
+            cnt = [k for dst, _, _, k in _sender_calls(cores, route, topo, s) if dst == core][0]
         else:
-            cnt = _engines(topo.mask(c, core), FWD_ENGINES)[1]
+            cnt = [k for dst, _, k in _forward(cores, route, topo, s, c) if dst == core][0]
         return ("arr%d" % s, cnt)
 
     def mat(s):
@@ -181,24 +211,25 @@ def rank_program(g, core, T, topo):
         ops.append((lhsT, rhs, wide, ps, sb))
         return sb, [("cp%d" % i, 1)]
 
-    a0 = [arrival(0)]
-    p = product((T.l0[:, 0:P], a0), (T.l0[:, P:W0], a0), False)
+    if rank == 0:
+        p = product(mat(0), (T.xs[:], [arrival(0)]), False)
+    else:
+        p = (T.l0[:], [arrival(0)])
+    fold = rank % 2 == 1 and rank >= 7
     pairs = []
     for j in range(1, rank // 2 + 1):
-        if rank % 2 and 2 * j == rank - 1 and rank >= 7:
+        if fold and 2 * j == rank - 1:
             pairs.append(product(mat(2 * j), mat(2 * j - 1), True))
         else:
             pairs.append(product(mat(2 * j - 1), mat(2 * j), True))
-    tail_done = False
     for j, b in enumerate(pairs):
-        if rank % 2 and rank >= 7 and j == len(pairs) - 1:
+        if fold and j == len(pairs) - 1:
             p = product(tail, p, False)
-            tail_done = True
             break
         p = product(b, p, False)
-        if rank % 2 and rank >= 7 and j == 0:
+        if fold and j == 0:
             tail = product(pairs[-1], mat(rank), True)
-    if rank % 2 and not tail_done:
+    if rank % 2 == 1 and not fold:
         p = product(mat(rank), p, False)
 
     seen = set()
@@ -210,6 +241,19 @@ def rank_program(g, core, T, topo):
         g.tensor.matmul(ps, lhsT[0], rhs[0], start=True, stop=True).then_inc(T.sem["mm%d" % i], 1)
         g.vector.wait_ge(T.sem["mm%d" % i], 1)
         g.vector.tensor_copy(sb, ps).then_inc(T.sem["cp%d" % i], 1)
+
+    sent = 0
+    if rank < n - 1:
+        if rank == 0:
+            g.wait_ge(T.sem[p[1][0][0]], 1)
+        else:
+            g.wait_ge(T.sem.staged, 16)
+        for dst, relay, mask, cnt in _sender_calls(cores, route, topo, rank):
+            if rank == 0:
+                write(0, p[0], T.l0[:], dst, mask)
+            else:
+                write(rank, T.d[:], T.d[:] if relay else _landing(T, rank), dst, mask)
+            sent += cnt
 
     g.sync.wait_ge(T.sem[p[1][0][0]], 1)
     g.sync.dma_start(T.y[:], p[0]).then_inc(T.sem.stored, 16)

from concourse.bass import DstId, RemoteDMATransfer

P, F = 128, 32
ENGINES = 8
SHARES = {1: [(0, 2)], 2: [(0, 2), (1, 3)], 3: [(0, 2), (1,), (3,)], 4: [(0,), (2,), (1,), (3,)]}

SCRATCH = {
    "d": ("dram", [P, P], "bfloat16"),
    "l0": ("sbuf", [P, F], "bfloat16"),
    "xs": ("sbuf", [P, F], "bfloat16"),
    "lm": ("sbuf", [P, 6 * P], "bfloat16"),
    "own": ("sbuf", [P, P], "bfloat16"),
    "pr": ("sbuf", [P, 4 * P], "bfloat16"),
    "pv": ("sbuf", [P, 4 * F], "bfloat16"),
    "pn": ("psum", [P, 512], "float32"),
    "pw0": ("psum", [P, 512], "float32"),
    "pw1": ("psum", [P, 512], "float32"),
    "pw2": ("psum", [P, 512], "float32"),
    "pw3": ("psum", [P, 512], "float32"),
}
SEMAPHORES = (["arr%d" % s for s in range(7)] + ["mm%d" % i for i in range(8)] + ["cp%d" % i for i in range(8)]
              + ["staged", "mine", "sent", "stored"])

_CACHE = {}


def _chip(topo, c):
    return (topo.host(c), topo.chip(c))


def _mate(topo, a):
    base = topo.host(a) * topo.CORES_PER_HOST
    for c in range(base + a % topo.CORES_PER_CHIP, base + topo.CORES_PER_HOST, topo.CORES_PER_CHIP):
        if topo.mates(a, c):
            return c


def _inrack(topo, a, b, die):
    if _chip(topo, a) == _chip(topo, b):
        return []
    if topo.same_plane(a, b):
        return [("out", _chip(topo, a), die), ("in", _chip(topo, b), die)]
    return [("mate", _chip(topo, a), die)] + _inrack(topo, _mate(topo, a), b, die)


def _way(topo, a, b):
    die = topo.die(a)
    if topo.rack(topo.host(a)) == topo.rack(topo.host(b)):
        return _inrack(topo, a, b, die)
    far = topo.host(b) * topo.CORES_PER_HOST + a % topo.CORES_PER_HOST
    near = topo.host(a) * topo.CORES_PER_HOST + b % topo.CORES_PER_HOST
    links = [("cable", _chip(topo, a), die)] + _inrack(topo, far, b, die)
    if _chip(topo, near) != _chip(topo, a):
        links += _inrack(topo, a, near, die) + [("cable", _chip(topo, near), die)]
    return links


def _plan(cores, topo):
    n = len(cores)
    world = range((max(topo.host(c) for c in cores) + 1) * topo.CORES_PER_HOST)
    used = set(cores)
    route, first, second, groups = {}, {}, {}, []

    def fits(s, ds, c):
        return c not in used and topo.may_write(cores[s], c) and all(topo.may_write(c, cores[d]) for d in ds)

    for s in range(n - 1):
        size = (F if s == 0 else P) * P * 2
        near, far = [], []
        for d in range(n - 1, s, -1):
            if topo.may_write(cores[s], cores[d]):
                route[(s, d)] = None
                for k in _way(topo, cores[s], cores[d]):
                    first[k] = first.get(k, 0) + size
            elif any(fits(s, [d], c) and _chip(topo, c) == _chip(topo, cores[s]) for c in world):
                near.append(d)
            else:
                far.append(d)
        for cls, ds in ((0, near), (1, far)):
            for grp in ([ds] if s == 0 else [[d] for d in ds]):
                if grp:
                    groups.append((cls, sum(1 for c in world if fits(s, grp, c)), -grp[0], s, grp, size))
    for _, _, _, s, grp, size in sorted(groups):
        a = cores[s]
        best = None
        for c in world:
            if not fits(s, grp, c):
                continue
            w1 = _way(topo, a, c)
            w2 = [k for d in grp for k in _way(topo, c, cores[d])]
            busy = max([first.get(k, 0) for k in w1] + [0]) + max(second.get(k, 0) for k in w2)
            key = (topo.die(c) != topo.die(a), _chip(topo, c) != _chip(topo, a),
                   topo.rack(topo.host(c)) != topo.rack(topo.host(a)), len(w1) + len(w2), busy, c)
            if best is None or key < best[0]:
                best = (key, w1, w2)
        c = best[0][-1]
        used.add(c)
        for d in grp:
            route[(s, d)] = c
        for k in best[1]:
            first[k] = first.get(k, 0) + size
        for k in best[2]:
            second[k] = second.get(k, 0) + size
    return route


def _bits(topo, src, dsts):
    mask = topo.mask(src, dsts[0])
    for c in dsts[1:]:
        mask &= topo.mask(src, c)
    bits, bit = [], 1
    while bit <= mask and len(bits) < ENGINES:
        if mask & bit:
            bits.append(bit)
        bit <<= 1
    return bits


def _together(topo, src, dsts, whole):
    bits = _bits(topo, src, dsts)
    if (whole and len(dsts) == 1) or len(dsts) not in SHARES:
        return [(c, sum(bits), len(bits)) for c in dsts]
    out = []
    for c, quarters in zip(dsts, SHARES[len(dsts)]):
        own = [b for q in quarters for b in bits[q::4]]
        out.append((c, sum(own), len(own)))
    return out


def _sender_calls(cores, route, topo, s):
    via, straight = [], []
    for d in range(len(cores) - 1, s, -1):
        c = route[(s, d)]
        if c is None:
            straight.append(cores[d])
        elif c not in via:
            via.append(c)
    calls = [(c, True, m, k) for c, m, k in (_together(topo, cores[s], via, False) if via else [])]
    for c in straight:
        bits = _bits(topo, cores[s], [c])
        calls.append((c, False, sum(bits), len(bits)))
    return calls


def _forward(cores, route, topo, s, c):
    return _together(topo, c, [cores[d] for d in range(len(cores) - 1, s, -1) if route[(s, d)] == c], True)


def _landing(T, s):
    return T.l0[:] if s == 0 else T.lm[:, (s - 1) * P:s * P]


def rank_program(g, core, T, topo):
    cores = list(T.cores)
    if "route" not in _CACHE:
        _CACHE["route"] = _plan(cores, topo)
    route = _CACHE["route"]
    n = len(cores)
    rank = T.rank_of(core)

    def write(s, src, out, dst, mask):
        rid, pid = topo.addr(dst, core)
        g.remote_dma(out, src, T.sem["arr%d" % s], T.sem.sent, pid, rid, mask)

    if rank is None:
        for s in sorted(set(s for (s, d), c in route.items() if c == core)):
            got = [k for c, _, _, k in _sender_calls(cores, route, topo, s) if c == core][0]
            g.wait_ge(T.sem["arr%d" % s], got)
            sent = 0
            for dst, mask, cnt in _forward(cores, route, topo, s, core):
                write(s, T.l0[:] if s == 0 else T.d[:], _landing(T, s), dst, mask)
                sent += cnt
            g.wait_ge(T.sem.sent, sent)
        return

    mine = 16
    if rank == 0:
        g.sync.dma_start(T.own[:], T.m[:]).then_inc(T.sem.mine, 16)
        g.scalar.dma_start(T.xs[:], T.x[:]).then_inc(T.sem.mine, 16)
        mine = 32
    else:
        if rank < n - 1:
            g.sync.dma_start(T.d[:], (T.mt if rank % 2 else T.m)[:]).then_inc(T.sem.staged, 16)
            g.scalar.wait_ge(T.sem.staged, 16)
        g.scalar.dma_start(T.own[:], T.m[:]).then_inc(T.sem.mine, 16)

    def arrival(s):
        if s == rank:
            return ("mine", mine)
        c = route[(s, rank)]
        if c is None:
            cnt = [k for dst, _, _, k in _sender_calls(cores, route, topo, s) if dst == core][0]
        else:
            cnt = [k for dst, _, k in _forward(cores, route, topo, s, c) if dst == core][0]
        return ("arr%d" % s, cnt)

    def mat(s):
        if s == rank:
            return T.own[:], [arrival(s)]
        return T.lm[:, (s - 1) * P:s * P], [arrival(s)]

    ops = []

    def product(lhsT, rhs, wide):
        i = len(ops)
        k = sum(1 for o in ops if o[2] == wide)
        if wide:
            ps, sb = T["pw%d" % k][:, 0:P], T.pr[:, k * P:(k + 1) * P]
        else:
            ps, sb = T.pn[:, 0:F], T.pv[:, k * F:(k + 1) * F]
        ops.append((lhsT, rhs, wide, ps, sb))
        return sb, [("cp%d" % i, 1)]

    if rank == 0:
        p = product(mat(0), (T.xs[:], [arrival(0)]), False)
    else:
        p = (T.l0[:], [arrival(0)])
    fold = rank % 2 == 1 and rank >= 7
    pairs = []
    for j in range(1, rank // 2 + 1):
        if fold and 2 * j == rank - 1:
            pairs.append(product(mat(2 * j), mat(2 * j - 1), True))
        else:
            pairs.append(product(mat(2 * j - 1), mat(2 * j), True))
    for j, b in enumerate(pairs):
        if fold and j == len(pairs) - 1:
            p = product(tail, p, False)
            break
        p = product(b, p, False)
        if fold and j == 0:
            tail = product(pairs[-1], mat(rank), True)
    if rank % 2 == 1 and not fold:
        p = product(mat(rank), p, False)

    seen = set()
    for i, (lhsT, rhs, wide, ps, sb) in enumerate(ops):
        for w in lhsT[1] + rhs[1]:
            if w not in seen:
                seen.add(w)
                g.tensor.wait_ge(T.sem[w[0]], w[1])
        g.tensor.matmul(ps, lhsT[0], rhs[0], start=True, stop=True).then_inc(T.sem["mm%d" % i], 1)
        g.vector.wait_ge(T.sem["mm%d" % i], 1)
        g.vector.tensor_copy(sb, ps).then_inc(T.sem["cp%d" % i], 1)

    sent = 0
    if rank < n - 1:
        if rank == 0:
            g.wait_ge(T.sem[p[1][0][0]], 1)
        else:
            g.wait_ge(T.sem.staged, 16)
        for dst, relay, mask, cnt in _sender_calls(cores, route, topo, rank):
            if rank == 0:
                write(0, p[0], T.l0[:], dst, mask)
            else:
                write(rank, T.d[:], T.d[:] if relay else _landing(T, rank), dst, mask)
            sent += cnt

    g.sync.wait_ge(T.sem[p[1][0][0]], 1)
    g.sync.dma_start(T.y[:], p[0]).then_inc(T.sem.stored, 16)
    g.sync.wait_ge(T.sem.stored, 16)
    if sent:
        g.wait_ge(T.sem.sent, sent)
